import numpy as np, ml_dtypes
CORES = [33,38,57,62,81,86,161,166,185,190,209,214]
N = 12
R, W, T = 4096, 128, 256
CAPP = 64
def entries(a): return a.T.reshape(-1)
def pack(v, P): return np.ascontiguousarray(np.asarray(v, np.int32).reshape(-1, P).T)
def lists(rng, how):
    Q = rng.permutation(N * R)[:N * T]
    if how == "hotrank": Q = R * int(rng.integers(N)) + rng.permutation(R)[:N * T]
    if how == "own": Q = np.concatenate([R * r + rng.permutation(R)[:T] for r in range(N)])
    if how == "sorted": Q = np.sort(Q)
    if how == "edge":
        ends = np.concatenate([R * np.arange(N), R * np.arange(N) + R - 1]); rest = np.setdiff1d(rng.permutation(N * R), ends, assume_unique=True)
        Q = rng.permutation(np.concatenate([ends, rng.permutation(rest)[:N * T - 2 * N]]))
    if how in ("uniform", "full", "sorted", "edge"):
        O = np.stack([rng.permutation(np.repeat(rng.permutation(N)[:T // CAPP], CAPP)) if how == "full" else rng.permutation(np.repeat(np.arange(N), CAPP))[:T] for r in range(N)]).reshape(-1); Q = np.zeros(N * T, np.int64)
        for d in range(N):
            m = np.nonzero(O == d)[0]; w = rng.permutation(R)[:len(m)]
            if how == "edge" and len(m) >= 2: w[:2] = [0, R - 1]; w[2:] = 1 + rng.permutation(R - 2)[:len(m) - 2]
            Q[m] = R * d + w
        if how == "sorted": Q = np.sort(Q.reshape(N, T), axis=1).reshape(-1)
    return {"pos": np.stack([pack(q, 128) for q in Q.reshape(N, T)])}
def setup_inputs(rng):
    return dict({"tab": rng.standard_normal((N, R, W), dtype=np.float32).astype(ml_dtypes.bfloat16), "new": rng.standard_normal((N, T, W), dtype=np.float32).astype(ml_dtypes.bfloat16)}, **lists(rng, "uniform"))
def setup_inputs_edge(rng):
    d = setup_inputs(rng); d.update(lists(rng, "edge"))
    for k in ("tab", "new"): d[k] = (d[k].astype(np.float32) * 1048576.0).astype(d[k].dtype)
    return d
def setup_inputs_full(rng):
    d = setup_inputs(rng); d.update(lists(rng, "full"))
    for k in ("tab", "new"): d[k] = (d[k].astype(np.float32) * (1 / 1024.0)).astype(d[k].dtype)
    return d
def setup_inputs_sorted(rng):
    d = setup_inputs(rng); d.update(lists(rng, "sorted"))
    return d
def check_inputs(x):
    bad = []
    if x["pos"].min() < 0 or x["pos"].max() >= N * R: bad.append("pos out of range")
    if len(np.unique(x["pos"])) != x["pos"].size: bad.append("a place is named twice")
    if max(int(np.bincount(entries(a) // R, minlength=N).max()) for a in x["pos"]) > CAPP: bad.append("more than CAPP entries of a list point into one rank's part")
    return bad
def reference(tab, new, pos):
    A = np.concatenate(list(tab), axis=0)
    for r in range(N): A[entries(pos[r])] = new[r]
    return {"y": np.stack([A[R * r:R * r + R] for r in range(N)])}

@@ -1,0 +1,269 @@
+from concourse.bass import DstId, RemoteDMATransfer, IndirectOffsetOnAxis
+from concourse.mybir import AluOpType, AxisListType
+
+R, W, CAP = 4096, 128, 64
+MW = 72
+TW = 2 * MW
+
+SCRATCH = {
+    "posS": ("sbuf", [128, 2], "int32"),
+    "newS": ("sbuf", [128, 256], "bfloat16"),
+    "I6": ("sbuf", [128, 6], "int32"),
+    "F6": ("sbuf", [128, 6], "float32"),
+    "d64": ("sbuf", [128, 2], "float32"),
+    "ones": ("sbuf", [128, 128], "bfloat16"),
+    "half": ("sbuf", [128, 128], "bfloat16"),
+    "tri": ("sbuf", [128, 128], "bfloat16"),
+    "ident": ("sbuf", [128, 128], "bfloat16"),
+    "io24": ("sbuf", [128, 24], "bfloat16"),
+    "io128": ("sbuf", [128, 128], "bfloat16"),
+    "DD": ("sbuf", [128, 36], "bfloat16"),
+    "Mx": ("sbuf", [128, 24], "float32"),
+    "slot": ("sbuf", [128, 2], "float32"),
+    "HL": ("sbuf", [128, 48], "bfloat16"),
+    "RR": ("sbuf", [128, 256], "bfloat16"),
+    "P": ("sbuf", [128, 1536], "bfloat16"),
+    "msg": ("sbuf", [128, 12 * MW], "bfloat16"),
+    "land": ("sbuf", [128, 6 * TW], "bfloat16"),
+    "rows": ("sbuf", [128, 6 * 128], "bfloat16"),
+    "idx": ("sbuf", [128, 6], "int32"),
+    "rl": ("sbuf", [128, 2 * TW], "bfloat16"),
+    "ps0": ("psum", [128, 512], "float32"),
+    "ps1": ("psum", [128, 512], "float32"),
+    "ps2": ("psum", [128, 512], "float32"),
+    "ps3": ("psum", [128, 512], "float32"),
+    "ps4": ("psum", [128, 512], "float32"),
+    "ps5": ("psum", [128, 512], "float32"),
+    "ps6": ("psum", [128, 512], "float32"),
+    "ps7": ("psum", [128, 512], "float32"),
+}
+SEMAPHORES = ["ldp", "ldn", "cpy", "gcp", "gcon", "vs", "ts", "sent", "sc", "rs0", "rs1",
+              "arr0", "arr1", "arr2", "arr3", "arr4", "arr5"]
+
+
+def _bits(m):
+    return [b for b in range(32) if (m >> b) & 1]
+
+
+def _mk(bs):
+    m = 0
+    for b in bs:
+        m |= 1 << b
+    return m
+
+
+def _plan(T, topo):
+    cores = list(T.cores)
+    place = lambda c: (topo.host(c), topo.chip(c))
+    chips = []
+    for c in cores:
+        if place(c) not in chips:
+            chips.append(place(c))
+    nc = len(chips)
+    mem = [[r for r, c in enumerate(cores) if place(c) == ch] for ch in chips]
+    for k in range(nc):
+        assert mem[k] == [2 * k, 2 * k + 1]
+    direct = lambda a, Rc: all(topo.may_write(cores[a], cores[b]) for b in mem[Rc])
+    cross = lambda Sc, Rc: not all(direct(a, Rc) for a in mem[Sc])
+    recv = []
+    for Rc in range(nc):
+        oth = [Sc for Sc in range(nc) if Sc != Rc]
+        recv.append([Rc] + sorted([s for s in oth if not cross(s, Rc)], key=lambda s: (s - Rc) % nc)
+                    + sorted([s for s in oth if cross(s, Rc)], key=lambda s: (s - Rc) % nc))
+    send = []
+    for Sc in range(nc):
+        oth = [Rc for Rc in range(nc) if Rc != Sc]
+        send.append([Sc] + sorted(oth, key=lambda r: recv[r].index(Sc) * 1.72 - (3.0 if cross(Sc, r) else 0.0)))
+    world = (max(topo.host(c) for c in cores) + 1) * topo.CORES_PER_HOST
+    jobs, via = {}, {}
+    for Sc in range(nc):
+        for a in mem[Sc]:
+            cand = [c for c in range(world) if place(c) == chips[Sc] and T.rank_of(c) is None
+                    and topo.die(c) == topo.die(cores[a]) and all(topo.may_write(c, d) for d in cores)]
+            for Rc in send[Sc][1:]:
+                if direct(a, Rc):
+                    continue
+                rc = min(cand, key=lambda c: len(jobs.get(c, [])))
+                jobs.setdefault(rc, [])
+                via[(a, Rc)] = (rc, len(jobs[rc]))
+                jobs[rc].append((a, Rc))
+                assert len(jobs[rc]) <= 2
+    return {"cores": cores, "mem": mem, "recv": recv, "send": send, "jobs": jobs, "via": via}
+
+
+def _pair(g, T, topo, core, pl, a, Rc, src, col):
+    cores, mem = pl["cores"], pl["mem"]
+    Sc, q = a // 2, a % 2
+    eng = [b for b in _bits(topo.mask(core, cores[mem[Rc][0]])) if b in _bits(topo.mask(core, cores[mem[Rc][1]]))][:8]
+    tr = []
+    for e, b in enumerate(mem[Rc]):
+        rid, pid = topo.addr(cores[b], core)
+        tr.append(RemoteDMATransfer(dst_ids=[DstId(rid=rid, pnc=pid)], dma_engine_mask=_mk(eng[4 * e:4 * e + 4]),
+                                    remote_sem=T.sem["arr%d" % Sc], src=src[:, col + MW * e:col + MW * e + MW],
+                                    dst=T.land[:, TW * Sc + MW * q:TW * Sc + MW * q + MW]))
+    g.remote_dma_fused(tr, local_sem=T.sem.sent)
+
+
+def _relay(g, core, T, topo, pl):
+    for s, (a, Rc) in enumerate(pl["jobs"][core]):
+        g.wait_ge(T.sem["rs%d" % s], 8)
+        _pair(g, T, topo, core, pl, a, Rc, T.rl, TW * s)
+    g.wait_ge(T.sem.sent, 8 * len(pl["jobs"][core]))
+
+
+def rank_program(g, core, T, topo):
+    pl = _plan(T, topo)
+    if core in pl["jobs"]:
+        _relay(g, core, T, topo, pl)
+        return
+    me = T.rank_of(core)
+    if me is None:
+        return
+    S, A = T.sem, AluOpType
+    v, pe = g.vector, g.tensor
+    cores = pl["cores"]
+    my, q = me // 2, me % 2
+    io = lambda h: 0 if h == 0 else CAP
+    do = lambda h: 8 if h == 0 else 0
+    n = {"v": 0, "t": 0}
+    bank = [T.ps2, T.ps3, T.ps4, T.ps5, T.ps6, T.ps7]
+
+    def V(ins):
+        ins.then_inc(S.vs, 1)
+        n["v"] += 1
+
+    def vw():
+        v.wait_ge(S.vs, n["v"])
+
+    def MM(out, lhsT, rhs, start, stop):
+        pe.matmul(out, lhsT, rhs, start, stop).then_inc(S.ts, 1)
+        n["t"] += 1
+
+    g.sync.dma_start(T.posS[:], T.pos[:]).then_inc(S.ldp, 16)
+    g.scalar.dma_start(T.newS[:, 0:128], T.new[0:128, :]).then_inc(S.ldn, 16)
+    g.sync.dma_start(T.newS[:, 128:256], T.new[128:256, :]).then_inc(S.ldn, 16)
+    g.sync.dma_start(T.y[0:1536, :], T.tab[0:1536, :]).then_inc(S.cpy, 16)
+    g.scalar.dma_start(T.y[1536:3072, :], T.tab[1536:3072, :]).then_inc(S.cpy, 16)
+
+    V(v.memset(T.ones[:], 1.0))
+    V(v.memset(T.half[:], 0.5))
+    V(v.memset(T.DD[:, 0:12], 0.0))
+    V(v.memset(T.msg[:], 0.0))
+    g.iota(T.io24[:], [[0, 2], [1, 12]], 0, 0, allow_small_or_imprecise_dtypes=True).then_inc(S.gcon, 1)
+    g.wait_ge(S.vs, 1)
+    g.affine_select(T.tri[:], T.ones[:], [[1, 128]], A.is_gt, 0.0, 0, -1).then_inc(S.gcon, 1)
+    g.iota(T.io128[:], [[1, 128]], 0, 0, allow_small_or_imprecise_dtypes=True).then_inc(S.gcon, 1)
+    g.affine_select(T.ident[:], T.ones[:], [[-1, 128]], A.is_equal, 0.0, 0, 1).then_inc(S.gcon, 1)
+    g.dma_start(T.y[3072:4096, :], T.tab[3072:4096, :]).then_inc(S.gcp, 16)
+
+    v.wait_ge(S.ldp, 16)
+    V(v.tensor_scalar(T.I6[:, 0:2], T.posS[:], 12, None, A.arith_shift_right))
+    V(v.tensor_scalar(T.I6[:, 2:4], T.posS[:], 6, 63, A.logical_shift_right, A.bitwise_and))
+    V(v.tensor_scalar(T.I6[:, 4:6], T.posS[:], 63, None, A.bitwise_and))
+    vw()
+    V(v.tensor_scalar(T.F6[:], T.I6[:], 1.0, None, A.add))
+    vw()
+    v.wait_ge(S.gcon, 1)
+    for k in range(2):
+        V(v.tensor_scalar(T.DD[:, 12 + 12 * k:24 + 12 * k], T.io24[:, 0:12], 1.0, T.F6[:, k:k + 1], A.add, A.is_equal))
+    cD = n["v"]
+    pe.wait_ge(S.vs, 2)
+    pe.wait_ge(S.gcon, 1)
+    MM(T.ps0[:, 0:24], T.half[:], T.io24[:], True, False)
+    pe.wait_ge(S.vs, cD)
+    pe.wait_ge(S.gcon, 2)
+    MM(T.ps0[:, 0:24], T.tri[:], T.DD[:, 12:36], False, False)
+    MM(T.ps0[:, 0:24], T.ones[:], T.DD[:, 0:24], False, True)
+    cS = n["t"]
+    V(v.tensor_scalar(T.d64[:], T.F6[:, 0:2], 64.0, -64.0 * (1 + q), A.mult, A.add))
+    vw()
+    for k in range(2):
+        for c in range(2):
+            V(v.tensor_scalar(T.HL[:, 24 * k + 12 * c:24 * k + 12 * c + 12], T.DD[:, 12 + 12 * k:24 + 12 * k],
+                              T.F6[:, 2 + 2 * c + k:3 + 2 * c + k], None, A.mult))
+    v.wait_ge(S.ts, cS)
+    V(v.tensor_tensor(T.Mx[:], T.DD[:, 12:36], T.ps0[:, 0:24], A.mult))
+    vw()
+    for k in range(2):
+        V(v.tensor_reduce(T.slot[:, k:k + 1], T.Mx[:, 12 * k:12 * k + 12], AxisListType.X, A.add))
+    vw()
+    v.wait_ge(S.gcon, 3)
+    for k in range(2):
+        V(v.tensor_scalar(T.RR[:, 128 * k:128 * k + 128], T.io128[:], T.d64[:, k:k + 1], T.slot[:, k:k + 1], A.add, A.is_equal))
+    cR = n["v"]
+    order = pl["send"][my]
+    cT = {}
+
+    def onehot(i):
+        gq = order[i]
+        for k in range(2):
+            V(v.tensor_scalar(T.P[:, 768 * k + 128 * gq:768 * k + 128 * gq + 128], T.io128[:], float(128 * gq),
+                              T.slot[:, k:k + 1], A.add, A.is_equal))
+        pe.wait_ge(S.vs, n["v"])
+        for k in range(2):
+            MM(bank[i][:, 0:128], T.newS[:, 128 * k:128 * k + 128], T.P[:, 768 * k + 128 * gq:768 * k + 128 * gq + 128],
+               k == 0, k == 1)
+        cT[i] = n["t"]
+
+    pe.wait_ge(S.vs, cR)
+    for k in range(2):
+        MM(T.ps1[:, 0:24], T.RR[:, 128 * k:128 * k + 128], T.HL[:, 24 * k:24 * k + 24], k == 0, k == 1)
+    cI = n["t"]
+    pe.wait_ge(S.ldn, 32)
+    onehot(0)
+    onehot(1)
+    v.wait_ge(S.ts, cI)
+    for c in range(2):
+        V(v.tensor_scalar(T.msg[:, io(q) + c:12 * MW:MW], T.ps1[:, 12 * c:12 * c + 12], -1.0, None, A.add))
+    sent = 0
+    for i, Rc in enumerate(order):
+        v.wait_ge(S.ts, cT[i])
+        for e in range(2):
+            d = 2 * Rc + e
+            dst = T.land[:, TW * my + MW * q + do(q):TW * my + MW * q + do(q) + CAP] if d == me \
+                else T.msg[:, MW * d + do(q):MW * d + do(q) + CAP]
+            V(v.tensor_copy(dst, bank[i][:, CAP * e:CAP * e + CAP]))
+        g.wait_ge(S.vs, n["v"])
+        if Rc == my:
+            p = 2 * my + 1 - q
+            rid, pid = topo.addr(cores[p], core)
+            g.remote_dma(T.land[:, TW * my + MW * q:TW * my + MW * q + MW], T.msg[:, MW * p:MW * p + MW],
+                         S["arr%d" % my], S.sent, pid, rid, _mk(_bits(topo.mask(core, cores[p]))[:8]))
+        elif (me, Rc) in pl["via"]:
+            rc, s = pl["via"][(me, Rc)]
+            rid, pid = topo.addr(rc, core)
+            g.remote_dma(T.rl[:, TW * s:TW * s + TW], T.msg[:, TW * Rc:TW * Rc + TW],
+                         S["rs%d" % s], S.sent, pid, rid, _mk(_bits(topo.mask(core, rc))[:8]))
+        else:
+            _pair(g, T, topo, core, pl, me, Rc, T.msg, TW * Rc)
+        sent += 8
+        if i + 2 < len(order):
+            onehot(i + 2)
+    cE = n["v"]
+
+    pe.wait_ge(S.vs, cE)
+    pe.wait_ge(S.gcon, 4)
+    g.wait_ge(S.cpy, 32)
+    g.wait_ge(S.gcp, 16)
+    for t, c in enumerate(pl["recv"][my]):
+        arr, need = S["arr%d" % c], 8
+        pe.wait_ge(arr, need)
+        MM(bank[t][:, 0:128], T.land[:, TW * c + 8:TW * c + 136], T.ident[:], True, True)
+        v.wait_ge(arr, need)
+        for h in range(2):
+            src, col = (T.msg, MW * me + io(q)) if (c == my and h == q) else (T.land, TW * c + MW * h + io(h))
+            V(v.tensor_scalar(T.idx[64 * h:64 * h + 64, t:t + 1], src[64 * h:64 * h + 64, col:col + 1], 64.0,
+                              src[64 * h:64 * h + 64, col + 1:col + 2], A.mult, A.add))
+        v.wait_ge(S.ts, n["t"])
+        V(v.tensor_copy(T.rows[:, 128 * t:128 * t + 128], bank[t][:, 0:128]))
+        g.wait_ge(arr, need)
+        g.wait_ge(S.vs, n["v"])
+        g.indirect_dma_start(out=T.y[:], out_offset=IndirectOffsetOnAxis(ap=T.idx[:, t:t + 1], axis=0),
+                             in_=T.rows[:, 128 * t:128 * t + 128], in_offset=None,
+                             bounds_check=R - 1, oob_is_err=False).then_inc(S.sc, 16)
+    g.wait_ge(S.sc, 16 * 6)
+    g.wait_ge(S.sent, sent)
+    g.wait_ge(S.ts, n["t"])
+    g.wait_ge(S.gcon, 4)
+    g.wait_ge(S.ldp, 16)
+    g.wait_ge(S.ldn, 32)

@@ -1,13 +1,19 @@
 from concourse.bass import DstId, RemoteDMATransfer, IndirectOffsetOnAxis
-from concourse.mybir import AluOpType, AxisListType
+from concourse.mybir import AluOpType, AxisListType, ActivationFunctionType
 
 R, W, CAP = 4096, 128, 64
 MW = 72
 TW = 2 * MW
+PW = 136
 
 SCRATCH = {
     "posS": ("sbuf", [128, 2], "int32"),
     "newS": ("sbuf", [128, 256], "bfloat16"),
+    "newP": ("sbuf", [128, 256], "bfloat16"),
+    "pmS": ("sbuf", [128, PW], "bfloat16"),
+    "pmL": ("sbuf", [128, 192], "bfloat16"),
+    "cb": ("sbuf", [128, 2], "bfloat16"),
+    "Oh": ("sbuf", [128, 256], "bfloat16"),
     "I6": ("sbuf", [128, 6], "int32"),
     "F6": ("sbuf", [128, 6], "float32"),
     "d64": ("sbuf", [128, 2], "float32"),
@@ -37,7 +43,7 @@ SCRATCH = {
     "ps6": ("psum", [128, 512], "float32"),
     "ps7": ("psum", [128, 512], "float32"),
 }
-SEMAPHORES = ["ldp", "ldn", "cpy", "gcp", "gcon", "vs", "ts", "sent", "sc", "rs0", "rs1",
+SEMAPHORES = ["ldp", "ldn", "cpy", "gcp", "gcon", "vs", "ts", "acs", "sent", "sc", "rs0", "rs1", "arn",
               "arr0", "arr1", "arr2", "arr3", "arr4", "arr5"]
 
 
@@ -120,12 +126,15 @@ def rank_program(g, core, T, topo):
     if me is None:
         return
     S, A = T.sem, AluOpType
-    v, pe = g.vector, g.tensor
+    v, pe, sc = g.vector, g.tensor, g.scalar
     cores = pl["cores"]
     my, q = me // 2, me % 2
+    p = 2 * my + 1 - q
+    prid, ppid = topo.addr(cores[p], core)
+    pmask = _mk(_bits(topo.mask(core, cores[p]))[:8])
     io = lambda h: 0 if h == 0 else CAP
     do = lambda h: 8 if h == 0 else 0
-    n = {"v": 0, "t": 0}
+    n = {"v": 0, "t": 0, "a": 0}
     bank = [T.ps2, T.ps3, T.ps4, T.ps5, T.ps6, T.ps7]
 
     def V(ins):
@@ -140,26 +149,33 @@ def rank_program(g, core, T, topo):
         n["t"] += 1
 
     g.sync.dma_start(T.posS[:], T.pos[:]).then_inc(S.ldp, 16)
-    g.scalar.dma_start(T.newS[:, 0:128], T.new[0:128, :]).then_inc(S.ldn, 16)
+    sc.dma_start(T.newS[:, 0:128], T.new[0:128, :]).then_inc(S.ldn, 16)
     g.sync.dma_start(T.newS[:, 128:256], T.new[128:256, :]).then_inc(S.ldn, 16)
     g.sync.dma_start(T.y[0:1536, :], T.tab[0:1536, :]).then_inc(S.cpy, 16)
-    g.scalar.dma_start(T.y[1536:3072, :], T.tab[1536:3072, :]).then_inc(S.cpy, 16)
+    sc.dma_start(T.y[1536:3072, :], T.tab[1536:3072, :]).then_inc(S.cpy, 16)
 
     V(v.memset(T.ones[:], 1.0))
     V(v.memset(T.half[:], 0.5))
     V(v.memset(T.DD[:, 0:12], 0.0))
     V(v.memset(T.msg[:], 0.0))
+    V(v.memset(T.pmS[:, 128:PW], 0.0))
+    V(v.memset(T.pmL[:, PW:192], 0.0))
+    V(v.memset(T.cb[:, 0:1], 0.0))
+    V(v.memset(T.cb[:, 1:2], -65.0 / 64.0))
+    cM = n["v"]
     g.iota(T.io24[:], [[0, 2], [1, 12]], 0, 0, allow_small_or_imprecise_dtypes=True).then_inc(S.gcon, 1)
     g.wait_ge(S.vs, 1)
     g.affine_select(T.tri[:], T.ones[:], [[1, 128]], A.is_gt, 0.0, 0, -1).then_inc(S.gcon, 1)
     g.iota(T.io128[:], [[1, 128]], 0, 0, allow_small_or_imprecise_dtypes=True).then_inc(S.gcon, 1)
-    g.affine_select(T.ident[:], T.ones[:], [[-1, 128]], A.is_equal, 0.0, 0, 1).then_inc(S.gcon, 1)
     g.dma_start(T.y[3072:4096, :], T.tab[3072:4096, :]).then_inc(S.gcp, 16)
+    g.wait_ge(S.ldn, 32)
+    g.remote_dma(T.newP[:], T.newS[:], S.arn, S.sent, ppid, prid, pmask)
+    g.affine_select(T.ident[:], T.ones[:], [[-1, 128]], A.is_equal, 0.0, 0, 1).then_inc(S.gcon, 1)
 
     v.wait_ge(S.ldp, 16)
     V(v.tensor_scalar(T.I6[:, 0:2], T.posS[:], 12, None, A.arith_shift_right))
-    V(v.tensor_scalar(T.I6[:, 2:4], T.posS[:], 6, 63, A.logical_shift_right, A.bitwise_and))
-    V(v.tensor_scalar(T.I6[:, 4:6], T.posS[:], 63, None, A.bitwise_and))
+    V(v.tensor_scalar(T.I6[:, 2:6:2], T.posS[:], 6, 63, A.logical_shift_right, A.bitwise_and))
+    V(v.tensor_scalar(T.I6[:, 3:6:2], T.posS[:], 63, None, A.bitwise_and))
     vw()
     V(v.tensor_scalar(T.F6[:], T.I6[:], 1.0, None, A.add))
     vw()
@@ -175,12 +191,13 @@ def rank_program(g, core, T, topo):
     MM(T.ps0[:, 0:24], T.tri[:], T.DD[:, 12:36], False, False)
     MM(T.ps0[:, 0:24], T.ones[:], T.DD[:, 0:24], False, True)
     cS = n["t"]
+    V(v.tensor_copy(T.pmS[:, 128:132], T.F6[:, 2:6]))
     V(v.tensor_scalar(T.d64[:], T.F6[:, 0:2], 64.0, -64.0 * (1 + q), A.mult, A.add))
     vw()
     for k in range(2):
         for c in range(2):
             V(v.tensor_scalar(T.HL[:, 24 * k + 12 * c:24 * k + 12 * c + 12], T.DD[:, 12 + 12 * k:24 + 12 * k],
-                              T.F6[:, 2 + 2 * c + k:3 + 2 * c + k], None, A.mult))
+                              T.F6[:, 2 + 2 * k + c:3 + 2 * k + c], None, A.mult))
     v.wait_ge(S.ts, cS)
     V(v.tensor_tensor(T.Mx[:], T.DD[:, 12:36], T.ps0[:, 0:24], A.mult))
     vw()
@@ -189,8 +206,12 @@ def rank_program(g, core, T, topo):
     vw()
     v.wait_ge(S.gcon, 3)
     for k in range(2):
+        V(v.tensor_scalar(T.pmS[:, CAP * k:CAP * k + CAP], T.io128[:, 0:CAP], float(CAP * p), T.slot[:, k:k + 1], A.add, A.is_equal))
+    g.wait_ge(S.vs, n["v"])
+    g.remote_dma(T.pmL[:, 0:PW], T.pmS[:], S["arr%d" % my], S.sent, ppid, prid, pmask)
+    sent = 16
+    for k in range(2):
         V(v.tensor_scalar(T.RR[:, 128 * k:128 * k + 128], T.io128[:], T.d64[:, k:k + 1], T.slot[:, k:k + 1], A.add, A.is_equal))
-    cR = n["v"]
     order = pl["send"][my]
     cT = {}
 
@@ -205,31 +226,29 @@ def rank_program(g, core, T, topo):
                k == 0, k == 1)
         cT[i] = n["t"]
 
-    pe.wait_ge(S.vs, cR)
+    pe.wait_ge(S.vs, n["v"])
     for k in range(2):
         MM(T.ps1[:, 0:24], T.RR[:, 128 * k:128 * k + 128], T.HL[:, 24 * k:24 * k + 24], k == 0, k == 1)
     cI = n["t"]
     pe.wait_ge(S.ldn, 32)
-    onehot(0)
     onehot(1)
+    onehot(2)
     v.wait_ge(S.ts, cI)
     for c in range(2):
         V(v.tensor_scalar(T.msg[:, io(q) + c:12 * MW:MW], T.ps1[:, 12 * c:12 * c + 12], -1.0, None, A.add))
-    sent = 0
-    for i, Rc in enumerate(order):
-        v.wait_ge(S.ts, cT[i])
+    cX = n["v"]
+    sc.wait_ge(S.vs, cM)
+    for i in range(1, len(order)):
+        Rc = order[i]
+        sc.wait_ge(S.ts, cT[i])
         for e in range(2):
             d = 2 * Rc + e
-            dst = T.land[:, TW * my + MW * q + do(q):TW * my + MW * q + do(q) + CAP] if d == me \
-                else T.msg[:, MW * d + do(q):MW * d + do(q) + CAP]
-            V(v.tensor_copy(dst, bank[i][:, CAP * e:CAP * e + CAP]))
-        g.wait_ge(S.vs, n["v"])
-        if Rc == my:
-            p = 2 * my + 1 - q
-            rid, pid = topo.addr(cores[p], core)
-            g.remote_dma(T.land[:, TW * my + MW * q:TW * my + MW * q + MW], T.msg[:, MW * p:MW * p + MW],
-                         S["arr%d" % my], S.sent, pid, rid, _mk(_bits(topo.mask(core, cores[p]))[:8]))
-        elif (me, Rc) in pl["via"]:
+            sc.activation(T.msg[:, MW * d + do(q):MW * d + do(q) + CAP], bank[i][:, CAP * e:CAP * e + CAP],
+                          ActivationFunctionType.Copy).then_inc(S.acs, 1)
+            n["a"] += 1
+        g.wait_ge(S.vs, cX)
+        g.wait_ge(S.acs, n["a"])
+        if (me, Rc) in pl["via"]:
             rc, s = pl["via"][(me, Rc)]
             rid, pid = topo.addr(rc, core)
             g.remote_dma(T.rl[:, TW * s:TW * s + TW], T.msg[:, TW * Rc:TW * Rc + TW],
@@ -239,24 +258,48 @@ def rank_program(g, core, T, topo):
         sent += 8
         if i + 2 < len(order):
             onehot(i + 2)
-    cE = n["v"]
 
-    pe.wait_ge(S.vs, cE)
+    for k in range(2):
+        V(v.tensor_scalar(T.Oh[:, 128 * k:128 * k + 128], T.io128[:], float(CAP * me - CAP), T.slot[:, k:k + 1], A.add, A.is_equal))
+    bA, bB = T.ps2, T.ps0
+    pe.wait_ge(S.vs, n["v"])
+    MM(bA[:, 128:130], T.half[:], T.cb[:], True, False)
+    for k in range(2):
+        MM(bA[:, 128:130], T.Oh[:, 128 * k:128 * k + 128], T.pmS[:, 128 + 2 * k:130 + 2 * k], False, k == 1)
+    for k in range(2):
+        MM(bA[:, 0:128], T.Oh[:, 128 * k:128 * k + 128], T.newS[:, 128 * k:128 * k + 128], k == 0, k == 1)
+    v.wait_ge(S.ts, n["t"])
+    V(v.tensor_scalar(T.idx[64:128, 0:1], bA[64:128, 128:129], 64.0, bA[64:128, 129:130], A.mult, A.add))
+    V(v.tensor_copy(T.rows[64:128, 0:128], bA[64:128, 0:128]))
+    MM(bB[:, 128:130], T.half[:], T.cb[:], True, False)
+    pe.wait_ge(S["arr%d" % my], 8)
+    for k in range(2):
+        MM(bB[:, 128:130], T.pmL[:, CAP * k:CAP * k + 128], T.pmL[:, 128 + 2 * k:130 + 2 * k], False, k == 1)
+    pe.wait_ge(S.arn, 8)
+    for k in range(2):
+        MM(bB[:, 0:128], T.pmL[:, CAP * k:CAP * k + 128], T.newP[:, 128 * k:128 * k + 128], k == 0, k == 1)
+    v.wait_ge(S.ts, n["t"])
+    V(v.tensor_scalar(T.idx[0:64, 0:1], bB[0:64, 128:129], 64.0, bB[0:64, 129:130], A.mult, A.add))
+    V(v.tensor_copy(T.rows[0:64, 0:128], bB[0:64, 0:128]))
+
+    pe.wait_ge(S.acs, n["a"])
     pe.wait_ge(S.gcon, 4)
     g.wait_ge(S.cpy, 32)
     g.wait_ge(S.gcp, 16)
+    g.wait_ge(S.arn, 8)
     for t, c in enumerate(pl["recv"][my]):
-        arr, need = S["arr%d" % c], 8
-        pe.wait_ge(arr, need)
-        MM(bank[t][:, 0:128], T.land[:, TW * c + 8:TW * c + 136], T.ident[:], True, True)
-        v.wait_ge(arr, need)
-        for h in range(2):
-            src, col = (T.msg, MW * me + io(q)) if (c == my and h == q) else (T.land, TW * c + MW * h + io(h))
-            V(v.tensor_scalar(T.idx[64 * h:64 * h + 64, t:t + 1], src[64 * h:64 * h + 64, col:col + 1], 64.0,
-                              src[64 * h:64 * h + 64, col + 1:col + 2], A.mult, A.add))
-        v.wait_ge(S.ts, n["t"])
-        V(v.tensor_copy(T.rows[:, 128 * t:128 * t + 128], bank[t][:, 0:128]))
-        g.wait_ge(arr, need)
+        arr = S["arr%d" % c]
+        if t > 0:
+            pe.wait_ge(arr, 8)
+            MM(bank[t][:, 0:128], T.land[:, TW * c + 8:TW * c + 136], T.ident[:], True, True)
+            v.wait_ge(arr, 8)
+            for h in range(2):
+                col = TW * c + MW * h + io(h)
+                V(v.tensor_scalar(T.idx[64 * h:64 * h + 64, t:t + 1], T.land[64 * h:64 * h + 64, col:col + 1], 64.0,
+                                  T.land[64 * h:64 * h + 64, col + 1:col + 2], A.mult, A.add))
+            v.wait_ge(S.ts, n["t"])
+            V(v.tensor_copy(T.rows[:, 128 * t:128 * t + 128], bank[t][:, 0:128]))
+        g.wait_ge(arr, 8)
         g.wait_ge(S.vs, n["v"])
         g.indirect_dma_start(out=T.y[:], out_offset=IndirectOffsetOnAxis(ap=T.idx[:, t:t + 1], axis=0),
                              in_=T.rows[:, 128 * t:128 * t + 128], in_offset=None,
@@ -266,4 +309,3 @@ def rank_program(g, core, T, topo):
     g.wait_ge(S.ts, n["t"])
     g.wait_ge(S.gcon, 4)
     g.wait_ge(S.ldp, 16)
-    g.wait_ge(S.ldn, 32)

from concourse.bass import DstId, RemoteDMATransfer, IndirectOffsetOnAxis
from concourse.mybir import AluOpType, AxisListType, ActivationFunctionType

R, W, CAP = 4096, 128, 64
MW = 72
TW = 2 * MW
PW = 136

SCRATCH = {
    "posS": ("sbuf", [128, 2], "int32"),
    "newS": ("sbuf", [128, 256], "bfloat16"),
    "newP": ("sbuf", [128, 256], "bfloat16"),
    "pmS": ("sbuf", [128, PW], "bfloat16"),
    "pmL": ("sbuf", [128, 192], "bfloat16"),
    "cb": ("sbuf", [128, 2], "bfloat16"),
    "Oh": ("sbuf", [128, 256], "bfloat16"),
    "I6": ("sbuf", [128, 6], "int32"),
    "F6": ("sbuf", [128, 6], "float32"),
    "d64": ("sbuf", [128, 2], "float32"),
    "ones": ("sbuf", [128, 128], "bfloat16"),
    "half": ("sbuf", [128, 128], "bfloat16"),
    "tri": ("sbuf", [128, 128], "bfloat16"),
    "ident": ("sbuf", [128, 128], "bfloat16"),
    "io24": ("sbuf", [128, 24], "bfloat16"),
    "io128": ("sbuf", [128, 128], "bfloat16"),
    "DD": ("sbuf", [128, 36], "bfloat16"),
    "Mx": ("sbuf", [128, 24], "float32"),
    "slot": ("sbuf", [128, 2], "float32"),
    "HL": ("sbuf", [128, 48], "bfloat16"),
    "RR": ("sbuf", [128, 256], "bfloat16"),
    "P": ("sbuf", [128, 1536], "bfloat16"),
    "msg": ("sbuf", [128, 12 * MW], "bfloat16"),
    "land": ("sbuf", [128, 6 * TW], "bfloat16"),
    "rows": ("sbuf", [128, 6 * 128], "bfloat16"),
    "idx": ("sbuf", [128, 6], "int32"),
    "rl": ("sbuf", [128, 2 * TW], "bfloat16"),
    "ps0": ("psum", [128, 512], "float32"),
    "ps1": ("psum", [128, 512], "float32"),
    "ps2": ("psum", [128, 512], "float32"),
    "ps3": ("psum", [128, 512], "float32"),
    "ps4": ("psum", [128, 512], "float32"),
    "ps5": ("psum", [128, 512], "float32"),
    "ps6": ("psum", [128, 512], "float32"),
    "ps7": ("psum", [128, 512], "float32"),
}
SEMAPHORES = ["ldp", "ldn", "cpy", "gcp", "gcon", "vs", "ts", "acs", "sent", "sc", "rs0", "rs1", "arn",
              "arr0", "arr1", "arr2", "arr3", "arr4", "arr5"]


def _bits(m):
    return [b for b in range(32) if (m >> b) & 1]


def _mk(bs):
    m = 0
    for b in bs:
        m |= 1 << b
    return m


def _plan(T, topo):
    cores = list(T.cores)
    place = lambda c: (topo.host(c), topo.chip(c))
    chips = []
    for c in cores:
        if place(c) not in chips:
            chips.append(place(c))
    nc = len(chips)
    mem = [[r for r, c in enumerate(cores) if place(c) == ch] for ch in chips]
    for k in range(nc):
        assert mem[k] == [2 * k, 2 * k + 1]
    direct = lambda a, Rc: all(topo.may_write(cores[a], cores[b]) for b in mem[Rc])
    cross = lambda Sc, Rc: not all(direct(a, Rc) for a in mem[Sc])
    recv = []
    for Rc in range(nc):
        oth = [Sc for Sc in range(nc) if Sc != Rc]
        recv.append([Rc] + sorted([s for s in oth if not cross(s, Rc)], key=lambda s: (s - Rc) % nc)
                    + sorted([s for s in oth if cross(s, Rc)], key=lambda s: (s - Rc) % nc))
    send = []
    for Sc in range(nc):
        oth = [Rc for Rc in range(nc) if Rc != Sc]
        send.append([Sc] + sorted(oth, key=lambda r: recv[r].index(Sc) * 1.72 - (3.0 if cross(Sc, r) else 0.0)))
    world = (max(topo.host(c) for c in cores) + 1) * topo.CORES_PER_HOST
    jobs, via = {}, {}
    for Sc in range(nc):
        for a in mem[Sc]:
            cand = [c for c in range(world) if place(c) == chips[Sc] and T.rank_of(c) is None
                    and topo.die(c) == topo.die(cores[a]) and all(topo.may_write(c, d) for d in cores)]
            for Rc in send[Sc][1:]:
                if direct(a, Rc):
                    continue
                rc = min(cand, key=lambda c: len(jobs.get(c, [])))
                jobs.setdefault(rc, [])
                via[(a, Rc)] = (rc, len(jobs[rc]))
                jobs[rc].append((a, Rc))
                assert len(jobs[rc]) <= 2
    return {"cores": cores, "mem": mem, "recv": recv, "send": send, "jobs": jobs, "via": via}


def _pair(g, T, topo, core, pl, a, Rc, src, col):
    cores, mem = pl["cores"], pl["mem"]
    Sc, q = a // 2, a % 2
    eng = [b for b in _bits(topo.mask(core, cores[mem[Rc][0]])) if b in _bits(topo.mask(core, cores[mem[Rc][1]]))][:8]
    tr = []
    for e, b in enumerate(mem[Rc]):
        rid, pid = topo.addr(cores[b], core)
        tr.append(RemoteDMATransfer(dst_ids=[DstId(rid=rid, pnc=pid)], dma_engine_mask=_mk(eng[4 * e:4 * e + 4]),
                                    remote_sem=T.sem["arr%d" % Sc], src=src[:, col + MW * e:col + MW * e + MW],
                                    dst=T.land[:, TW * Sc + MW * q:TW * Sc + MW * q + MW]))
    g.remote_dma_fused(tr, local_sem=T.sem.sent)


def _relay(g, core, T, topo, pl):
    for s, (a, Rc) in enumerate(pl["jobs"][core]):
        g.wait_ge(T.sem["rs%d" % s], 8)
        _pair(g, T, topo, core, pl, a, Rc, T.rl, TW * s)
    g.wait_ge(T.sem.sent, 8 * len(pl["jobs"][core]))


def rank_program(g, core, T, topo):
    pl = _plan(T, topo)
    if core in pl["jobs"]:
        _relay(g, core, T, topo, pl)
        return
    me = T.rank_of(core)
    if me is None:
        return
    S, A = T.sem, AluOpType
    v, pe, sc = g.vector, g.tensor, g.scalar
    cores = pl["cores"]
    my, q = me // 2, me % 2
    p = 2 * my + 1 - q
    prid, ppid = topo.addr(cores[p], core)
    pmask = _mk(_bits(topo.mask(core, cores[p]))[:8])
    io = lambda h: 0 if h == 0 else CAP
    do = lambda h: 8 if h == 0 else 0
    n = {"v": 0, "t": 0, "a": 0}
    bank = [T.ps2, T.ps3, T.ps4, T.ps5, T.ps6, T.ps7]

    def V(ins):
        ins.then_inc(S.vs, 1)
        n["v"] += 1

    def vw():
        v.wait_ge(S.vs, n["v"])

    def MM(out, lhsT, rhs, start, stop):
        pe.matmul(out, lhsT, rhs, start, stop).then_inc(S.ts, 1)
        n["t"] += 1

    g.sync.dma_start(T.posS[:], T.pos[:]).then_inc(S.ldp, 16)
    sc.dma_start(T.newS[:, 0:128], T.new[0:128, :]).then_inc(S.ldn, 16)
    g.sync.dma_start(T.newS[:, 128:256], T.new[128:256, :]).then_inc(S.ldn, 16)
    g.sync.dma_start(T.y[0:1536, :], T.tab[0:1536, :]).then_inc(S.cpy, 16)
    sc.dma_start(T.y[1536:3072, :], T.tab[1536:3072, :]).then_inc(S.cpy, 16)

    V(v.memset(T.ones[:], 1.0))
    V(v.memset(T.half[:], 0.5))
    V(v.memset(T.DD[:, 0:12], 0.0))
    V(v.memset(T.msg[:], 0.0))
    V(v.memset(T.pmS[:, 128:PW], 0.0))
    V(v.memset(T.pmL[:, PW:192], 0.0))
    V(v.memset(T.cb[:, 0:1], 0.0))
    V(v.memset(T.cb[:, 1:2], -65.0 / 64.0))
    cM = n["v"]
    g.iota(T.io24[:], [[0, 2], [1, 12]], 0, 0, allow_small_or_imprecise_dtypes=True).then_inc(S.gcon, 1)
    g.wait_ge(S.vs, 1)
    g.affine_select(T.tri[:], T.ones[:], [[1, 128]], A.is_gt, 0.0, 0, -1).then_inc(S.gcon, 1)
    g.iota(T.io128[:], [[1, 128]], 0, 0, allow_small_or_imprecise_dtypes=True).then_inc(S.gcon, 1)
    g.dma_start(T.y[3072:4096, :], T.tab[3072:4096, :]).then_inc(S.gcp, 16)
    g.wait_ge(S.ldn, 32)
    g.remote_dma(T.newP[:], T.newS[:], S.arn, S.sent, ppid, prid, pmask)
    g.affine_select(T.ident[:], T.ones[:], [[-1, 128]], A.is_equal, 0.0, 0, 1).then_inc(S.gcon, 1)

    v.wait_ge(S.ldp, 16)
    V(v.tensor_scalar(T.I6[:, 0:2], T.posS[:], 12, None, A.arith_shift_right))
    V(v.tensor_scalar(T.I6[:, 2:6:2], T.posS[:], 6, 63, A.logical_shift_right, A.bitwise_and))
    V(v.tensor_scalar(T.I6[:, 3:6:2], T.posS[:], 63, None, A.bitwise_and))
    vw()
    V(v.tensor_scalar(T.F6[:], T.I6[:], 1.0, None, A.add))
    vw()
    v.wait_ge(S.gcon, 1)
    for k in range(2):
        V(v.tensor_scalar(T.DD[:, 12 + 12 * k:24 + 12 * k], T.io24[:, 0:12], 1.0, T.F6[:, k:k + 1], A.add, A.is_equal))
    cD = n["v"]
    pe.wait_ge(S.vs, 2)
    pe.wait_ge(S.gcon, 1)
    MM(T.ps0[:, 0:24], T.half[:], T.io24[:], True, False)
    pe.wait_ge(S.vs, cD)
    pe.wait_ge(S.gcon, 2)
    MM(T.ps0[:, 0:24], T.tri[:], T.DD[:, 12:36], False, False)
    MM(T.ps0[:, 0:24], T.ones[:], T.DD[:, 0:24], False, True)
    cS = n["t"]
    V(v.tensor_copy(T.pmS[:, 128:132], T.F6[:, 2:6]))
    V(v.tensor_scalar(T.d64[:], T.F6[:, 0:2], 64.0, -64.0 * (1 + q), A.mult, A.add))
    vw()
    for k in range(2):
        for c in range(2):
            V(v.tensor_scalar(T.HL[:, 24 * k + 12 * c:24 * k + 12 * c + 12], T.DD[:, 12 + 12 * k:24 + 12 * k],
                              T.F6[:, 2 + 2 * k + c:3 + 2 * k + c], None, A.mult))
    v.wait_ge(S.ts, cS)
    V(v.tensor_tensor(T.Mx[:], T.DD[:, 12:36], T.ps0[:, 0:24], A.mult))
    vw()
    for k in range(2):
        V(v.tensor_reduce(T.slot[:, k:k + 1], T.Mx[:, 12 * k:12 * k + 12], AxisListType.X, A.add))
    vw()
    v.wait_ge(S.gcon, 3)
    for k in range(2):
        V(v.tensor_scalar(T.pmS[:, CAP * k:CAP * k + CAP], T.io128[:, 0:CAP], float(CAP * p), T.slot[:, k:k + 1], A.add, A.is_equal))
    g.wait_ge(S.vs, n["v"])
    g.remote_dma(T.pmL[:, 0:PW], T.pmS[:], S["arr%d" % my], S.sent, ppid, prid, pmask)
    sent = 16
    for k in range(2):
        V(v.tensor_scalar(T.RR[:, 128 * k:128 * k + 128], T.io128[:], T.d64[:, k:k + 1], T.slot[:, k:k + 1], A.add, A.is_equal))
    order = pl["send"][my]
    cT = {}

    def onehot(i):
        gq = order[i]
        for k in range(2):
            V(v.tensor_scalar(T.P[:, 768 * k + 128 * gq:768 * k + 128 * gq + 128], T.io128[:], float(128 * gq),
                              T.slot[:, k:k + 1], A.add, A.is_equal))
        pe.wait_ge(S.vs, n["v"])
        for k in range(2):
            MM(bank[i][:, 0:128], T.newS[:, 128 * k:128 * k + 128], T.P[:, 768 * k + 128 * gq:768 * k + 128 * gq + 128],
               k == 0, k == 1)
        cT[i] = n["t"]

    pe.wait_ge(S.vs, n["v"])
    for k in range(2):
        MM(T.ps1[:, 0:24], T.RR[:, 128 * k:128 * k + 128], T.HL[:, 24 * k:24 * k + 24], k == 0, k == 1)
    cI = n["t"]
    pe.wait_ge(S.ldn, 32)
    onehot(1)
    onehot(2)
    v.wait_ge(S.ts, cI)
    for c in range(2):
        V(v.tensor_scalar(T.msg[:, io(q) + c:12 * MW:MW], T.ps1[:, 12 * c:12 * c + 12], -1.0, None, A.add))
    cX = n["v"]
    sc.wait_ge(S.vs, cM)
    for i in range(1, len(order)):
        Rc = order[i]
        sc.wait_ge(S.ts, cT[i])
        for e in range(2):
            d = 2 * Rc + e
            sc.activation(T.msg[:, MW * d + do(q):MW * d + do(q) + CAP], bank[i][:, CAP * e:CAP * e + CAP],
                          ActivationFunctionType.Copy).then_inc(S.acs, 1)
            n["a"] += 1
        g.wait_ge(S.vs, cX)
        g.wait_ge(S.acs, n["a"])
        if (me, Rc) in pl["via"]:
            rc, s = pl["via"][(me, Rc)]
            rid, pid = topo.addr(rc, core)
            g.remote_dma(T.rl[:, TW * s:TW * s + TW], T.msg[:, TW * Rc:TW * Rc + TW],
                         S["rs%d" % s], S.sent, pid, rid, _mk(_bits(topo.mask(core, rc))[:8]))
        else:
            _pair(g, T, topo, core, pl, me, Rc, T.msg, TW * Rc)
        sent += 8
        if i + 2 < len(order):
            onehot(i + 2)

    for k in range(2):
        V(v.tensor_scalar(T.Oh[:, 128 * k:128 * k + 128], T.io128[:], float(CAP * me - CAP), T.slot[:, k:k + 1], A.add, A.is_equal))
    bA, bB = T.ps2, T.ps0
    pe.wait_ge(S.vs, n["v"])
    MM(bA[:, 128:130], T.half[:], T.cb[:], True, False)
    for k in range(2):
        MM(bA[:, 128:130], T.Oh[:, 128 * k:128 * k + 128], T.pmS[:, 128 + 2 * k:130 + 2 * k], False, k == 1)
    for k in range(2):
        MM(bA[:, 0:128], T.Oh[:, 128 * k:128 * k + 128], T.newS[:, 128 * k:128 * k + 128], k == 0, k == 1)
    v.wait_ge(S.ts, n["t"])
    V(v.tensor_scalar(T.idx[64:128, 0:1], bA[64:128, 128:129], 64.0, bA[64:128, 129:130], A.mult, A.add))
    V(v.tensor_copy(T.rows[64:128, 0:128], bA[64:128, 0:128]))
    MM(bB[:, 128:130], T.half[:], T.cb[:], True, False)
    pe.wait_ge(S["arr%d" % my], 8)
    for k in range(2):
        MM(bB[:, 128:130], T.pmL[:, CAP * k:CAP * k + 128], T.pmL[:, 128 + 2 * k:130 + 2 * k], False, k == 1)
    pe.wait_ge(S.arn, 8)
    for k in range(2):
        MM(bB[:, 0:128], T.pmL[:, CAP * k:CAP * k + 128], T.newP[:, 128 * k:128 * k + 128], k == 0, k == 1)
    v.wait_ge(S.ts, n["t"])
    V(v.tensor_scalar(T.idx[0:64, 0:1], bB[0:64, 128:129], 64.0, bB[0:64, 129:130], A.mult, A.add))
    V(v.tensor_copy(T.rows[0:64, 0:128], bB[0:64, 0:128]))

    pe.wait_ge(S.acs, n["a"])
    pe.wait_ge(S.gcon, 4)
    g.wait_ge(S.cpy, 32)
    g.wait_ge(S.gcp, 16)
    g.wait_ge(S.arn, 8)
    for t, c in enumerate(pl["recv"][my]):
        arr = S["arr%d" % c]
        if t > 0:
            pe.wait_ge(arr, 8)
            MM(bank[t][:, 0:128], T.land[:, TW * c + 8:TW * c + 136], T.ident[:], True, True)
            v.wait_ge(arr, 8)
            for h in range(2):
                col = TW * c + MW * h + io(h)
                V(v.tensor_scalar(T.idx[64 * h:64 * h + 64, t:t + 1], T.land[64 * h:64 * h + 64, col:col + 1], 64.0,
                                  T.land[64 * h:64 * h + 64, col + 1:col + 2], A.mult, A.add))
            v.wait_ge(S.ts, n["t"])
            V(v.tensor_copy(T.rows[:, 128 * t:128 * t + 128], bank[t][:, 0:128]))
        g.wait_ge(arr, 8)
        g.wait_ge(S.vs, n["v"])
        g.indirect_dma_start(out=T.y[:], out_offset=IndirectOffsetOnAxis(ap=T.idx[:, t:t + 1], axis=0),
                             in_=T.rows[:, 128 * t:128 * t + 128], in_offset=None,
                             bounds_check=R - 1, oob_is_err=False).then_inc(S.sc, 16)
    g.wait_ge(S.sc, 16 * 6)
    g.wait_ge(S.sent, sent)
    g.wait_ge(S.ts, n["t"])
    g.wait_ge(S.gcon, 4)
    g.wait_ge(S.ldp, 16)
